import numpy as np
import ml_dtypes


def mxq(x, axis, fmt="e4m3"):
    dtype, down = {"e4m3": (ml_dtypes.float8_e4m3fn, 7), "e5m2": (ml_dtypes.float8_e5m2, 14)}[fmt]
    v = np.moveaxis(np.asarray(x, np.float32).astype(ml_dtypes.bfloat16).astype(np.float64), axis, -1)
    blocks = v.reshape(v.shape[:-1] + (-1, 32))
    amax = np.abs(blocks).max(-1, keepdims=True)
    byte = np.maximum(np.where(amax > 0, np.frexp(amax)[1] - 1 + 127, 0) - down, 1)
    scale = np.exp2(byte - 127.0)
    codes = (blocks / scale).astype(np.float32).astype(dtype).astype(np.float64)
    return np.moveaxis((codes * scale).reshape(v.shape), -1, axis)


WIDE = False


def mx_kscale(k):
    if not WIDE:
        return np.ones(k)
    levels = np.array([10, -10, 5, -5, 0])
    if k % 512:
        return np.exp2(np.random.permutation(np.resize(levels, k // 32))).repeat(32)
    a = np.empty((k // 512, 16))
    for p in range(k // 512):
        a[p, :8] = np.random.permutation(np.resize(levels, 8))
        for g in range(8):
            far = levels[np.abs(levels - a[p, g]) >= 10]
            a[p, g + 8] = far[np.random.randint(len(far))]
    return np.exp2(a.ravel()).repeat(32)


def f64(x):
    return np.asarray(x).astype(np.float64)


def striped(idx):
    return np.tile(idx.reshape(-1, 16).T, (8, 1)).astype(np.uint16)


def unstriped(offs):
    return offs[:16].T.reshape(-1).astype(np.int64)


def pack_weight(w):
    k, n = w.shape
    w = f64(np.asarray(w, np.float32).astype(ml_dtypes.bfloat16)).reshape(k // 32, 32, n)
    amax = np.abs(w).max(1)
    byte = np.clip(np.where(amax > 0, np.frexp(amax)[1] - 1 + 127 - 7, 1), 1, 254)
    scaled = (w * np.exp2(127.0 - byte)[:, None, :]).reshape(k, n).astype(np.float32)
    words = np.ascontiguousarray(scaled.reshape(k // 512, 128, 4, n).transpose(0, 1, 3, 2)).astype(ml_dtypes.float8_e4m3fn).view(np.uint8)
    return words, np.ascontiguousarray(byte.astype(np.uint8).reshape(k // 512, 16, n))


def unpack_weight(words, scales):
    g, p, n, _ = words.shape
    vals = np.ascontiguousarray(words).view(ml_dtypes.float8_e4m3fn).astype(np.float64) * np.repeat(np.exp2(scales.astype(np.float64) - 127.0), 8, axis=1)[..., None]
    return vals.transpose(0, 1, 3, 2).reshape(g * 512, n)


def gelu(v):
    return 0.5 * v * (1.0 + np.tanh(np.sqrt(2.0 / np.pi) * (v + 0.044715 * v**3)))


K, T, E, C, N = 512, 768, 12, 128, 512


def by_expert(wq, xq):
    return np.concatenate([wq[e].T @ xq[:, e * C:(e + 1) * C] for e in range(E)], axis=1)


def setup_inputs():
    n = np.random.standard_normal
    s = mx_kscale(K)[:, None]
    first = np.random.permutation(np.repeat(np.arange(E), T // E))
    second = (first + 1 + np.random.permutation(np.repeat(np.arange(E - 1), -(-T // (E - 1)))[:T])) % E
    while np.bincount(second, minlength=E).max() != T // E:
        load = np.bincount(second, minlength=E); hi, lo = int(load.argmax()), int(load.argmin())
        t = np.flatnonzero((second == hi) & (first != lo))[0]; second[t] = lo
    slot_token = np.empty(E * C, np.int64); pos = np.empty((2, T), np.int64); fill = np.zeros(E, np.int64)
    place = np.stack([np.random.permutation(C) for _ in range(E)])
    for r, deal in enumerate((first, second)):
        for t in np.random.permutation(T):
            e = deal[t]; j = e * C + place[e, fill[e]]; fill[e] += 1; slot_token[j] = t; pos[r, t] = j
    g = np.random.uniform(0.2, 0.8, T)
    packed = [pack_weight(m) for m in n((E, K, N)) / np.sqrt(K) / s[None]]
    return {
        "xT": (n((K, T)) * s).astype(np.float32),
        "w_words": np.stack([m[0] for m in packed]),
        "w_scales": np.stack([m[1] for m in packed]),
        "b": (0.3 * n((N, E))).astype(np.float32),
        "gate": np.stack([np.tile(g, (N, 1)), np.tile(1.0 - g, (N, 1))]).astype(np.float32),
        "offs": striped(slot_token),
        "pos1": striped(pos[0]),
        "pos2": striped(pos[1]),
    }


def reference(xT, w_words, w_scales, b, gate, offs, pos1, pos2):
    idx = unstriped(offs)
    xq = mxq(f64(xT)[:, idx], 0, "e4m3")
    w = np.stack([unpack_weight(w_words[e], w_scales[e]) for e in range(E)])
    y = by_expert(w, xq)
    y = gelu(y + np.repeat(f64(b), C, axis=1))
    return f64(gate[0]) * y[:, unstriped(pos1)] + f64(gate[1]) * y[:, unstriped(pos2)]

@@ -1,0 +1,164 @@
+from contextlib import ExitStack
+
+import concourse.mybir as mybir
+from concourse.masks import make_identity
+
+K, T, E, C, N = 512, 768, 12, 128, 512
+FLOPS = 2 * E * C * K * N
+BYTES = 4 * K * T + E * K * N + E * (K // 32) * N + 4 * N * E + 2 * 4 * T + 2 * 2 * E * C + 4 * N * T
+
+F32 = mybir.dt.float32
+BF16 = mybir.dt.bfloat16
+I32 = mybir.dt.int32
+U32 = mybir.dt.uint32
+U16 = mybir.dt.uint16
+U8 = mybir.dt.uint8
+FP8X4 = mybir.dt.float8_e4m3fn_x4
+MULT = mybir.AluOpType.mult
+ADD = mybir.AluOpType.add
+COPY = mybir.ActivationFunctionType.Copy
+GELU = mybir.ActivationFunctionType.Gelu_apprx_tanh
+
+P = 128
+S = E * C
+NB = N // P
+CHUNK = 256
+CHUNKS = T // CHUNK
+WORD_CUTS = {0: 576, 576: 1152, 1152: 1536}
+SCALE_CUTS = ((0, 576, 0, 4), (576, 1152, 4, 9), (1152, 1408, 9, 11), (1408, 1536, 11, 12))
+LOADS = ((0, 4), (4, 8), (8, 12))
+
+
+def tile_routed_moe_kernel(tc, xT, w_words, w_scales, b, gate, offs, pos1, pos2, out):
+    nc = tc.nc
+    with ExitStack() as ctx:
+        keep = ctx.enter_context(tc.tile_pool(name="keep", bufs=1))
+        psum = ctx.enter_context(tc.psum_pool(name="psum", bufs=8))
+
+        offs_sb = keep.tile([P, S // 16], U16, name="offs_sb")
+        pos1_sb = keep.tile([P, T // 16], U16, name="pos1_sb")
+        pos2_sb = keep.tile([P, T // 16], U16, name="pos2_sb")
+        pos_sb = (pos1_sb, pos2_sb)
+
+        raw = [keep.tile([P, 4, CHUNK], F32, name=f"raw{c}", align_bytes=64) for c in range(CHUNKS)]
+        grouped = [keep.tile([P, CHUNK, 4], BF16, name=f"grouped{c}", align_bytes=64) for c in range(CHUNKS)]
+        words = keep.tile([P, T], U32, name="words", align_bytes=64)
+        scales = keep.tile([P, T], U8, name="scales", align_bytes=64)
+        slot_words = keep.tile([P, S], U32, name="slot_words", align_bytes=64)
+        slot_scales = keep.tile([P, S], U8, name="slot_scales", align_bytes=64)
+        w_sb = keep.tile([P, E, N], U32, name="w_sb", align_bytes=64)
+        ws_sb = keep.tile([P, E, N], U8, name="ws_sb", align_bytes=64)
+        b_sb = keep.tile([P, NB, E], F32, name="b_sb")
+        gate_sb = [keep.tile([P, T], F32, name=f"gate{r}") for r in range(2)]
+        y = [keep.tile([P, S], F32, name=f"y{nb}") for nb in range(NB)]
+        warm = keep.tile([P, 1], F32, name="warm")
+
+        nc.vector.memset(ws_sb[:].rearrange("p e n -> p (e n)").bitcast(I32), 0)
+        nc.gpsimd.memset(warm[:], 0.0)
+        nc.gpsimd.memset(scales[:], 0)
+        ident = keep.tile([P, P], F32, name="ident")
+        make_identity(nc, ident[:])
+        nc.scalar.activation(warm[:], warm[:], GELU)
+
+        x_rows = xT.rearrange("(p j) t -> p j t", j=4)
+        for c in range(CHUNKS):
+            nc.sync.dma_start(out=raw[c][:], in_=x_rows[:, :, c * CHUNK : (c + 1) * CHUNK])
+        nc.sync.dma_start(offs_sb[:], offs)
+        nc.scalar.dma_start(out=b_sb[:], in_=b.rearrange("(q p) e -> p q e", p=P))
+        for r in range(4):
+            nc.sync.dma_start(
+                out=ws_sb[r:P:32, :, :].bitcast(I32),
+                in_=w_scales[:, 0, r::4, :].rearrange("e q n -> q e n").bitcast(I32),
+            )
+
+        def load_weights(h):
+            for e0, e1 in LOADS:
+                cols = slice(h * 256, h * 256 + 256)
+                nc.sync.dma_start(
+                    out=w_sb[:, e0:e1, cols].bitcast(I32),
+                    in_=w_words[e0:e1, 0, :, cols, :].rearrange("e p n r -> p e (n r)").bitcast(I32),
+                )
+
+        load_weights(0)
+        nc.sync.dma_start(pos1_sb[:], pos1)
+        nc.sync.dma_start(pos2_sb[:], pos2)
+        for r in range(2):
+            nc.sync.dma_start(out=gate_sb[r][:], in_=gate[r, 0:P, :])
+        load_weights(1)
+
+        for c in range(CHUNKS):
+            cut = CHUNK if c < CHUNKS - 1 else 160
+            src = raw[c][:].rearrange("p j t -> p t j")
+            nc.vector.tensor_copy(out=grouped[c][:, 0:cut, :], in_=src[:, 0:cut, :])
+            if cut < CHUNK:
+                nc.scalar.copy(out=grouped[c][:, cut:CHUNK, :], in_=src[:, cut:CHUNK, :])
+            cols = slice(c * CHUNK, (c + 1) * CHUNK)
+            nc.vector.quantize_mx(
+                out=words[:, cols].bitcast(FP8X4),
+                scales=scales[:, cols],
+                in_=grouped[c][:].rearrange("p t j -> p (t j)"),
+            )
+
+        def experts(nbs, e0, e1):
+            accs = [psum.tile([P, 4 * C], F32, name=f"acc", tag="acc") for nb in nbs]
+            for nb, acc in zip(nbs, accs):
+                for e in range(e0, e1):
+                    feat = slice(nb * P, (nb + 1) * P)
+                    slots = slice(e * C, (e + 1) * C)
+                    nc.tensor.matmul_mx(
+                        out=acc[:, (e - e0) * C : (e - e0 + 1) * C],
+                        lhsT=w_sb[:, e, feat].bitcast(FP8X4),
+                        lhsT_scale=ws_sb[:, e, feat],
+                        rhs=slot_words[:, slots].bitcast(FP8X4),
+                        rhs_scale=slot_scales[:, slots],
+                        start=True,
+                        stop=True,
+                    )
+            for nb, acc in zip(nbs, accs):
+                for e in range(e0, e1):
+                    nc.scalar.activation(
+                        y[nb][:, e * C : (e + 1) * C],
+                        acc[:, (e - e0) * C : (e - e0 + 1) * C],
+                        GELU,
+                        bias=b_sb[:, nb, e : e + 1],
+                    )
+
+        def pick(dst, src, s0, s1):
+            nc.vector.tensor_copy(dst[:, s0:s1], src[:].indirect(offs_sb[:, s0 // 16 : s1 // 16]))
+
+        for s0, s1, e0, e1 in SCALE_CUTS:
+            if s0 in WORD_CUTS:
+                pick(slot_words, words, s0, WORD_CUTS[s0])
+            pick(slot_scales, scales, s0, s1)
+            for a in range(e0, e1, 4):
+                experts((0, 1), a, min(a + 4, e1))
+        for nbs in ((2,), (3,)):
+            for e0, e1 in LOADS:
+                experts(nbs, e0, e1)
+
+        def combine(nb, t0, t1):
+            n = t1 - t0
+            part = [keep.tile([P, n], F32, name=f"part{nb}_{t0}_{r}") for r in range(2)]
+            for r in range(2):
+                nc.vector.tensor_tensor(
+                    part[r][:],
+                    y[nb][:].indirect(pos_sb[r][:, t0 // 16 : t1 // 16]),
+                    gate_sb[r][:, t0:t1],
+                    MULT,
+                )
+            total = keep.tile([P, n], F32, name=f"total{nb}_{t0}")
+            on_pe = (T, 448, 0, 0)[nb]
+            for a in range(0, on_pe, 512):
+                z = min(a + 512, on_pe)
+                both = psum.tile([P, 4 * C], F32, name="both", tag="acc")
+                for r in range(2):
+                    nc.tensor.matmul(both[:, 0 : z - a], ident[:], part[r][:, a:z], start=(r == 0), stop=(r == 1))
+                nc.scalar.copy(total[:, a:z], both[:, 0 : z - a])
+            if on_pe < n:
+                nc.vector.tensor_tensor(total[:, on_pe:n], part[0][:, on_pe:n], part[1][:, on_pe:n], ADD)
+            nc.sync.dma_start(out=out[nb * P : (nb + 1) * P, t0:t1], in_=total[:])
+
+        for nb in range(NB - 1):
+            combine(nb, 0, T)
+        combine(NB - 1, 0, 512)
+        combine(NB - 1, 512, T)

@@ -47,13 +47,13 @@ def tile_routed_moe_kernel(tc, xT, w_words, w_scales, b, gate, offs, pos1, pos2,
         slot_words = keep.tile([P, S], U32, name="slot_words", align_bytes=64)
         slot_scales = keep.tile([P, S], U8, name="slot_scales", align_bytes=64)
         w_sb = keep.tile([P, E, N], U32, name="w_sb", align_bytes=64)
-        ws_sb = keep.tile([P, E, N], U8, name="ws_sb", align_bytes=64)
+        ws_sb = keep.tile([P, E // 4 * N], U8, name="ws_sb", align_bytes=64)
         b_sb = keep.tile([P, NB, E], F32, name="b_sb")
         gate_sb = [keep.tile([P, T], F32, name=f"gate{r}") for r in range(2)]
         y = [keep.tile([P, S], F32, name=f"y{nb}") for nb in range(NB)]
         warm = keep.tile([P, 1], F32, name="warm")
 
-        nc.vector.memset(ws_sb[:].rearrange("p e n -> p (e n)").bitcast(I32), 0)
+        nc.vector.memset(ws_sb[:].bitcast(I32), 0)
         nc.gpsimd.memset(warm[:], 0.0)
         nc.gpsimd.memset(scales[:], 0)
         ident = keep.tile([P, P], F32, name="ident")
@@ -64,34 +64,37 @@ def tile_routed_moe_kernel(tc, xT, w_words, w_scales, b, gate, offs, pos1, pos2,
         for c in range(CHUNKS):
             nc.sync.dma_start(out=raw[c][:], in_=x_rows[:, :, c * CHUNK : (c + 1) * CHUNK])
         nc.sync.dma_start(offs_sb[:], offs)
-        nc.scalar.dma_start(out=b_sb[:], in_=b.rearrange("(q p) e -> p q e", p=P))
-        for r in range(4):
-            nc.sync.dma_start(
-                out=ws_sb[r:P:32, :, :].bitcast(I32),
-                in_=w_scales[:, 0, r::4, :].rearrange("e q n -> q e n").bitcast(I32),
-            )
+        for g in range(E // 4):
+            for q in range(4):
+                nc.sync.dma_start(
+                    out=ws_sb[32 * q : 32 * q + 16, g * N : (g + 1) * N].bitcast(I32),
+                    in_=w_scales[4 * g : 4 * g + 4, 0, 4 * q : 4 * q + 4, :].bitcast(I32),
+                )
 
-        def load_weights(h):
-            for e0, e1 in LOADS:
-                cols = slice(h * 256, h * 256 + 256)
+        def load_weights(n0, n1, pieces):
+            for e0, e1 in pieces:
+                cols = slice(n0, n1)
                 nc.sync.dma_start(
                     out=w_sb[:, e0:e1, cols].bitcast(I32),
                     in_=w_words[e0:e1, 0, :, cols, :].rearrange("e p n r -> p e (n r)").bitcast(I32),
                 )
 
-        load_weights(0)
+        load_weights(0, 128, ((0, 6), (6, 12)))
+        nc.sync.dma_start(out=b_sb[:], in_=b.rearrange("(q p) e -> p q e", p=P))
         nc.sync.dma_start(pos1_sb[:], pos1)
         nc.sync.dma_start(pos2_sb[:], pos2)
         for r in range(2):
             nc.sync.dma_start(out=gate_sb[r][:], in_=gate[r, 0:P, :])
-        load_weights(1)
+        load_weights(128, 256, ((0, 12),))
+        load_weights(256, 512, ((0, 6), (6, 12)))
 
         for c in range(CHUNKS):
             cut = CHUNK if c < CHUNKS - 1 else 160
-            src = raw[c][:].rearrange("p j t -> p t j")
-            nc.vector.tensor_copy(out=grouped[c][:, 0:cut, :], in_=src[:, 0:cut, :])
+            src = raw[c][:].rearrange("p j (t i) -> p t j i", i=4)
+            dst = grouped[c][:].rearrange("p (t i) j -> p t j i", i=4)
+            nc.vector.tensor_copy(out=dst[:, 0 : cut // 4], in_=src[:, 0 : cut // 4])
             if cut < CHUNK:
-                nc.scalar.copy(out=grouped[c][:, cut:CHUNK, :], in_=src[:, cut:CHUNK, :])
+                nc.scalar.copy(out=dst[:, cut // 4 : CHUNK // 4], in_=src[:, cut // 4 : CHUNK // 4])
             cols = slice(c * CHUNK, (c + 1) * CHUNK)
             nc.vector.quantize_mx(
                 out=words[:, cols].bitcast(FP8X4),
@@ -108,7 +111,7 @@ def tile_routed_moe_kernel(tc, xT, w_words, w_scales, b, gate, offs, pos1, pos2,
                     nc.tensor.matmul_mx(
                         out=acc[:, (e - e0) * C : (e - e0 + 1) * C],
                         lhsT=w_sb[:, e, feat].bitcast(FP8X4),
-                        lhsT_scale=ws_sb[:, e, feat],
+                        lhsT_scale=ws_sb[4 * (e % 4) : P, e // 4 * N + nb * P : e // 4 * N + (nb + 1) * P],
                         rhs=slot_words[:, slots].bitcast(FP8X4),
                         rhs_scale=slot_scales[:, slots],
                         start=True,
@@ -131,23 +134,24 @@ def tile_routed_moe_kernel(tc, xT, w_words, w_scales, b, gate, offs, pos1, pos2,
                 pick(slot_words, words, s0, WORD_CUTS[s0])
             pick(slot_scales, scales, s0, s1)
             for a in range(e0, e1, 4):
-                experts((0, 1), a, min(a + 4, e1))
-        for nbs in ((2,), (3,)):
+                experts((0,), a, min(a + 4, e1))
+        for nbs in ((1,), (2,), (3,)):
             for e0, e1 in LOADS:
                 experts(nbs, e0, e1)
 
-        def combine(nb, t0, t1):
+        def fetch(nb, t0, t1, r):
+            part = keep.tile([P, t1 - t0], F32, name=f"part{nb}_{t0}_{r}")
+            nc.vector.tensor_tensor(
+                part[:],
+                y[nb][:].indirect(pos_sb[r][:, t0 // 16 : t1 // 16]),
+                gate_sb[r][:, t0:t1],
+                MULT,
+            )
+            return part
+
+        def finish(nb, t0, t1, on_pe, part):
             n = t1 - t0
-            part = [keep.tile([P, n], F32, name=f"part{nb}_{t0}_{r}") for r in range(2)]
-            for r in range(2):
-                nc.vector.tensor_tensor(
-                    part[r][:],
-                    y[nb][:].indirect(pos_sb[r][:, t0 // 16 : t1 // 16]),
-                    gate_sb[r][:, t0:t1],
-                    MULT,
-                )
             total = keep.tile([P, n], F32, name=f"total{nb}_{t0}")
-            on_pe = (T, 448, 0, 0)[nb]
             for a in range(0, on_pe, 512):
                 z = min(a + 512, on_pe)
                 both = psum.tile([P, 4 * C], F32, name="both", tag="acc")
@@ -158,7 +162,11 @@ def tile_routed_moe_kernel(tc, xT, w_words, w_scales, b, gate, offs, pos1, pos2,
                 nc.vector.tensor_tensor(total[:, on_pe:n], part[0][:, on_pe:n], part[1][:, on_pe:n], ADD)
             nc.sync.dma_start(out=out[nb * P : (nb + 1) * P, t0:t1], in_=total[:])
 
-        for nb in range(NB - 1):
-            combine(nb, 0, T)
-        combine(NB - 1, 0, 512)
-        combine(NB - 1, 512, T)
+        pieces = [(0, 0, T, T), (1, 0, T, 448), (2, 0, T, 0), (3, 0, 512, 0), (3, 512, T, 0)]
+        last = None
+        for piece in pieces:
+            first = fetch(*piece[:3], 0)
+            if last:
+                finish(*last)
+            last = (*piece, (first, fetch(*piece[:3], 1)))
+        finish(*last)

@@ -22,8 +22,8 @@ GELU = mybir.ActivationFunctionType.Gelu_apprx_tanh
 P = 128
 S = E * C
 NB = N // P
-CHUNK = 256
-CHUNKS = T // CHUNK
+CHUNKS = ((0, 384, 256), (384, 256, 160), (640, 128, 80))
+QUANTS = {0: ((0, 256), (256, 128)), 384: ((0, 256),), 640: ((0, 128),)}
 WORD_CUTS = {0: 576, 576: 1152, 1152: 1536}
 SCALE_CUTS = ((0, 576, 0, 4), (576, 1152, 4, 9), (1152, 1408, 9, 11), (1408, 1536, 11, 12))
 LOADS = ((0, 4), (4, 8), (8, 12))
@@ -40,8 +40,8 @@ def tile_routed_moe_kernel(tc, xT, w_words, w_scales, b, gate, offs, pos1, pos2,
         pos2_sb = keep.tile([P, T // 16], U16, name="pos2_sb")
         pos_sb = (pos1_sb, pos2_sb)
 
-        raw = [keep.tile([P, 4, CHUNK], F32, name=f"raw{c}", align_bytes=64) for c in range(CHUNKS)]
-        grouped = [keep.tile([P, CHUNK, 4], BF16, name=f"grouped{c}", align_bytes=64) for c in range(CHUNKS)]
+        raw = [keep.tile([P, 4, n], F32, name=f"raw{t0}", align_bytes=64) for t0, n, cut in CHUNKS]
+        grouped = [keep.tile([P, n, 4], BF16, name=f"grouped{t0}", align_bytes=64) for t0, n, cut in CHUNKS]
         words = keep.tile([P, T], U32, name="words", align_bytes=64)
         scales = keep.tile([P, T], U8, name="scales", align_bytes=64)
         slot_words = keep.tile([P, S], U32, name="slot_words", align_bytes=64)
@@ -61,8 +61,8 @@ def tile_routed_moe_kernel(tc, xT, w_words, w_scales, b, gate, offs, pos1, pos2,
         nc.scalar.activation(warm[:], warm[:], GELU)
 
         x_rows = xT.rearrange("(p j) t -> p j t", j=4)
-        for c in range(CHUNKS):
-            nc.sync.dma_start(out=raw[c][:], in_=x_rows[:, :, c * CHUNK : (c + 1) * CHUNK])
+        for c, (t0, n, cut) in enumerate(CHUNKS):
+            nc.sync.dma_start(out=raw[c][:], in_=x_rows[:, :, t0 : t0 + n])
         nc.sync.dma_start(offs_sb[:], offs)
         for g in range(E // 4):
             for q in range(4):
@@ -88,19 +88,18 @@ def tile_routed_moe_kernel(tc, xT, w_words, w_scales, b, gate, offs, pos1, pos2,
         load_weights(128, 256, ((0, 12),))
         load_weights(256, 512, ((0, 6), (6, 12)))
 
-        for c in range(CHUNKS):
-            cut = CHUNK if c < CHUNKS - 1 else 160
+        for c, (t0, n, cut) in enumerate(CHUNKS):
             src = raw[c][:].rearrange("p j (t i) -> p t j i", i=4)
             dst = grouped[c][:].rearrange("p (t i) j -> p t j i", i=4)
             nc.vector.tensor_copy(out=dst[:, 0 : cut // 4], in_=src[:, 0 : cut // 4])
-            if cut < CHUNK:
-                nc.scalar.copy(out=dst[:, cut // 4 : CHUNK // 4], in_=src[:, cut // 4 : CHUNK // 4])
-            cols = slice(c * CHUNK, (c + 1) * CHUNK)
-            nc.vector.quantize_mx(
-                out=words[:, cols].bitcast(FP8X4),
-                scales=scales[:, cols],
-                in_=grouped[c][:].rearrange("p t j -> p (t j)"),
-            )
+            nc.scalar.copy(out=dst[:, cut // 4 : n // 4], in_=src[:, cut // 4 : n // 4])
+            for q0, qn in QUANTS[t0]:
+                cols = slice(t0 + q0, t0 + q0 + qn)
+                nc.vector.quantize_mx(
+                    out=words[:, cols].bitcast(FP8X4),
+                    scales=scales[:, cols],
+                    in_=grouped[c][:, q0 : q0 + qn, :].rearrange("p t j -> p (t j)"),
+                )
 
         def experts(nbs, e0, e1):
             accs = [psum.tile([P, 4 * C], F32, name=f"acc", tag="acc") for nb in nbs]
@@ -162,11 +161,16 @@ def tile_routed_moe_kernel(tc, xT, w_words, w_scales, b, gate, offs, pos1, pos2,
                 nc.vector.tensor_tensor(total[:, on_pe:n], part[0][:, on_pe:n], part[1][:, on_pe:n], ADD)
             nc.sync.dma_start(out=out[nb * P : (nb + 1) * P, t0:t1], in_=total[:])
 
-        pieces = [(0, 0, T, T), (1, 0, T, 448), (2, 0, T, 0), (3, 0, 512, 0), (3, 512, T, 0)]
+        pieces = [(0, 0, T, T), (1, 0, T, 448), (2, 0, T, 0), (3, 0, 512, 0)]
         last = None
         for piece in pieces:
             first = fetch(*piece[:3], 0)
             if last:
                 finish(*last)
             last = (*piece, (first, fetch(*piece[:3], 1)))
+        ends = ((512, 640), (640, T))
+        firsts = [fetch(3, t0, t1, 0) for t0, t1 in ends]
         finish(*last)
+        seconds = [fetch(3, t0, t1, 1) for t0, t1 in ends]
+        for (t0, t1), first, second in zip(ends, firsts, seconds):
+            finish(3, t0, t1, 0, (first, second))

@@ -33,6 +33,7 @@ def tile_routed_moe_kernel(tc, xT, w_words, w_scales, b, gate, offs, pos1, pos2,
     nc = tc.nc
     with ExitStack() as ctx:
         keep = ctx.enter_context(tc.tile_pool(name="keep", bufs=1))
+        turns = ctx.enter_context(tc.tile_pool(name="turns", bufs=3))
         psum = ctx.enter_context(tc.psum_pool(name="psum", bufs=8))
 
         offs_sb = keep.tile([P, S // 16], U16, name="offs_sb")
@@ -64,29 +65,33 @@ def tile_routed_moe_kernel(tc, xT, w_words, w_scales, b, gate, offs, pos1, pos2,
         for c, (t0, n, cut) in enumerate(CHUNKS):
             nc.sync.dma_start(out=raw[c][:], in_=x_rows[:, :, t0 : t0 + n])
         nc.sync.dma_start(offs_sb[:], offs)
-        for g in range(E // 4):
+        def load_scales(g):
             for q in range(4):
                 nc.sync.dma_start(
                     out=ws_sb[32 * q : 32 * q + 16, g * N : (g + 1) * N].bitcast(I32),
                     in_=w_scales[4 * g : 4 * g + 4, 0, 4 * q : 4 * q + 4, :].bitcast(I32),
                 )
 
-        def load_weights(n0, n1, pieces):
-            for e0, e1 in pieces:
-                cols = slice(n0, n1)
-                nc.sync.dma_start(
-                    out=w_sb[:, e0:e1, cols].bitcast(I32),
-                    in_=w_words[e0:e1, 0, :, cols, :].rearrange("e p n r -> p e (n r)").bitcast(I32),
-                )
+        def load_weights(n0, n1, e0, e1):
+            cols = slice(n0, n1)
+            nc.sync.dma_start(
+                out=w_sb[:, e0:e1, cols].bitcast(I32),
+                in_=w_words[e0:e1, 0, :, cols, :].rearrange("e p n r -> p e (n r)").bitcast(I32),
+            )
 
-        load_weights(0, 128, ((0, 6), (6, 12)))
+        load_weights(0, P, 0, 4)
+        load_scales(0)
         nc.sync.dma_start(out=b_sb[:], in_=b.rearrange("(q p) e -> p q e", p=P))
+        load_weights(0, P, 4, E)
+        load_scales(1)
+        load_scales(2)
         nc.sync.dma_start(pos1_sb[:], pos1)
         nc.sync.dma_start(pos2_sb[:], pos2)
         for r in range(2):
             nc.sync.dma_start(out=gate_sb[r][:], in_=gate[r, 0:P, :])
-        load_weights(128, 256, ((0, 12),))
-        load_weights(256, 512, ((0, 6), (6, 12)))
+        load_weights(P, 2 * P, 0, E)
+        load_weights(2 * P, N, 0, 6)
+        load_weights(2 * P, N, 6, E)
 
         for c, (t0, n, cut) in enumerate(CHUNKS):
             src = raw[c][:].rearrange("p j (t i) -> p t j i", i=4)
@@ -148,20 +153,50 @@ def tile_routed_moe_kernel(tc, xT, w_words, w_scales, b, gate, offs, pos1, pos2,
             )
             return part
 
-        def finish(nb, t0, t1, on_pe, part):
-            n = t1 - t0
-            total = keep.tile([P, n], F32, name=f"total{nb}_{t0}")
-            for a in range(0, on_pe, 512):
-                z = min(a + 512, on_pe)
-                both = psum.tile([P, 4 * C], F32, name="both", tag="acc")
-                for r in range(2):
-                    nc.tensor.matmul(both[:, 0 : z - a], ident[:], part[r][:, a:z], start=(r == 0), stop=(r == 1))
-                nc.scalar.copy(total[:, a:z], both[:, 0 : z - a])
-            if on_pe < n:
-                nc.vector.tensor_tensor(total[:, on_pe:n], part[0][:, on_pe:n], part[1][:, on_pe:n], ADD)
-            nc.sync.dma_start(out=out[nb * P : (nb + 1) * P, t0:t1], in_=total[:])
+        def add_by_identity(part, a, z, total):
+            both = psum.tile([P, 4 * C], F32, name="both", tag="acc")
+            for r in range(2):
+                nc.tensor.matmul(both[:, 0 : z - a], ident[:], part[r][:, a:z], start=(r == 0), stop=(r == 1))
+            nc.scalar.copy(total[:, a:z], both[:, 0 : z - a])
 
-        pieces = [(0, 0, T, T), (1, 0, T, 448), (2, 0, T, 0), (3, 0, 512, 0)]
+        def add_turned(part, a, z):
+            turned = psum.tile([P, 4 * C], F32, name="turned", tag="acc")
+            for t in range(a, z, P):
+                for r in range(2):
+                    nc.tensor.matmul(
+                        turned[:, t - a : t - a + P], part[r][:, t : t + P], ident[:],
+                        start=(r == 0), stop=(r == 1), is_transpose=True,
+                    )
+            rows = turns.tile([P, 4 * C], F32, name="rows")
+            nc.scalar.copy(rows[:, 0 : z - a], turned[:, 0 : z - a])
+            return rows
+
+        def turn_back(rows, a, z, total):
+            both = psum.tile([P, 4 * C], F32, name="both", tag="acc")
+            for t in range(0, z - a, P):
+                nc.tensor.transpose(both[:, t : t + P], rows[:, t : t + P], ident[:])
+            nc.scalar.copy(total[:, a:z], both[:, 0 : z - a])
+
+        def finish(nb, t0, t1, ways, part):
+            total = keep.tile([P, t1 - t0], F32, name=f"total{nb}_{t0}")
+            turned = [add_turned(part, a, z) if way == "turn" else None for way, a, z in ways]
+            for rows, (way, a, z) in zip(turned, ways):
+                if way == "turn":
+                    turn_back(rows, a, z, total)
+                elif way == "identity":
+                    add_by_identity(part, a, z, total)
+                else:
+                    nc.vector.tensor_tensor(total[:, a:z], part[0][:, a:z], part[1][:, a:z], ADD)
+                queue = nc.sync if way == "vector" else nc.scalar
+                queue.dma_start(out=out[nb * P : (nb + 1) * P, t0 + a : t0 + z], in_=total[:, a:z])
+
+        pieces = [
+            (0, 0, T, [("identity", 0, 384), ("turn", 384, T)]),
+            (1, 0, T, [("turn", 0, 384), ("turn", 384, T)]),
+            (2, 0, 384, [("turn", 0, 384)]),
+            (2, 384, T, [("vector", 0, 384)]),
+            (3, 0, 512, [("vector", 0, 512)]),
+        ]
         last = None
         for piece in pieces:
             first = fetch(*piece[:3], 0)
@@ -173,4 +208,4 @@ def tile_routed_moe_kernel(tc, xT, w_words, w_scales, b, gate, offs, pos1, pos2,
         finish(*last)
         seconds = [fetch(3, t0, t1, 1) for t0, t1 in ends]
         for (t0, t1), first, second in zip(ends, firsts, seconds):
-            finish(3, t0, t1, 0, (first, second))
+            finish(3, t0, t1, [("vector", 0, t1 - t0)], (first, second))

from contextlib import ExitStack

import concourse.mybir as mybir
from concourse.masks import make_identity

K, T, E, C, N = 512, 768, 12, 128, 512
FLOPS = 2 * E * C * K * N
BYTES = 4 * K * T + E * K * N + E * (K // 32) * N + 4 * N * E + 2 * 4 * T + 2 * 2 * E * C + 4 * N * T

F32 = mybir.dt.float32
BF16 = mybir.dt.bfloat16
I32 = mybir.dt.int32
U32 = mybir.dt.uint32
U16 = mybir.dt.uint16
U8 = mybir.dt.uint8
FP8X4 = mybir.dt.float8_e4m3fn_x4
MULT = mybir.AluOpType.mult
ADD = mybir.AluOpType.add
COPY = mybir.ActivationFunctionType.Copy
GELU = mybir.ActivationFunctionType.Gelu_apprx_tanh

P = 128
S = E * C
NB = N // P
CHUNKS = ((0, 384, 256), (384, 256, 160), (640, 128, 80))
QUANTS = {0: ((0, 256), (256, 128)), 384: ((0, 256),), 640: ((0, 128),)}
WORD_CUTS = {0: 576, 576: 1152, 1152: 1536}
SCALE_CUTS = ((0, 576, 0, 4), (576, 1152, 4, 9), (1152, 1408, 9, 11), (1408, 1536, 11, 12))
LOADS = ((0, 4), (4, 8), (8, 12))


def tile_routed_moe_kernel(tc, xT, w_words, w_scales, b, gate, offs, pos1, pos2, out):
    nc = tc.nc
    with ExitStack() as ctx:
        keep = ctx.enter_context(tc.tile_pool(name="keep", bufs=1))
        turns = ctx.enter_context(tc.tile_pool(name="turns", bufs=3))
        psum = ctx.enter_context(tc.psum_pool(name="psum", bufs=8))

        offs_sb = keep.tile([P, S // 16], U16, name="offs_sb")
        pos1_sb = keep.tile([P, T // 16], U16, name="pos1_sb")
        pos2_sb = keep.tile([P, T // 16], U16, name="pos2_sb")
        pos_sb = (pos1_sb, pos2_sb)

        raw = [keep.tile([P, 4, n], F32, name=f"raw{t0}", align_bytes=64) for t0, n, cut in CHUNKS]
        grouped = [keep.tile([P, n, 4], BF16, name=f"grouped{t0}", align_bytes=64) for t0, n, cut in CHUNKS]
        words = keep.tile([P, T], U32, name="words", align_bytes=64)
        scales = keep.tile([P, T], U8, name="scales", align_bytes=64)
        slot_words = keep.tile([P, S], U32, name="slot_words", align_bytes=64)
        slot_scales = keep.tile([P, S], U8, name="slot_scales", align_bytes=64)
        w_sb = keep.tile([P, E, N], U32, name="w_sb", align_bytes=64)
        ws_sb = keep.tile([P, E // 4 * N], U8, name="ws_sb", align_bytes=64)
        b_sb = keep.tile([P, NB, E], F32, name="b_sb")
        gate_sb = [keep.tile([P, T], F32, name=f"gate{r}") for r in range(2)]
        y = [keep.tile([P, S], F32, name=f"y{nb}") for nb in range(NB)]
        warm = keep.tile([P, 1], F32, name="warm")

        nc.vector.memset(ws_sb[:].bitcast(I32), 0)
        nc.gpsimd.memset(warm[:], 0.0)
        nc.gpsimd.memset(scales[:], 0)
        ident = keep.tile([P, P], F32, name="ident")
        make_identity(nc, ident[:])
        nc.scalar.activation(warm[:], warm[:], GELU)

        x_rows = xT.rearrange("(p j) t -> p j t", j=4)
        for c, (t0, n, cut) in enumerate(CHUNKS):
            nc.sync.dma_start(out=raw[c][:], in_=x_rows[:, :, t0 : t0 + n])
        nc.sync.dma_start(offs_sb[:], offs)
        def load_scales(g):
            for q in range(4):
                nc.sync.dma_start(
                    out=ws_sb[32 * q : 32 * q + 16, g * N : (g + 1) * N].bitcast(I32),
                    in_=w_scales[4 * g : 4 * g + 4, 0, 4 * q : 4 * q + 4, :].bitcast(I32),
                )

        def load_weights(n0, n1, e0, e1):
            cols = slice(n0, n1)
            nc.sync.dma_start(
                out=w_sb[:, e0:e1, cols].bitcast(I32),
                in_=w_words[e0:e1, 0, :, cols, :].rearrange("e p n r -> p e (n r)").bitcast(I32),
            )

        load_weights(0, P, 0, 4)
        load_scales(0)
        nc.sync.dma_start(out=b_sb[:], in_=b.rearrange("(q p) e -> p q e", p=P))
        load_weights(0, P, 4, E)
        load_scales(1)
        load_scales(2)
        nc.sync.dma_start(pos1_sb[:], pos1)
        nc.sync.dma_start(pos2_sb[:], pos2)
        for r in range(2):
            nc.sync.dma_start(out=gate_sb[r][:], in_=gate[r, 0:P, :])
        load_weights(P, 2 * P, 0, E)
        load_weights(2 * P, N, 0, 6)
        load_weights(2 * P, N, 6, E)

        for c, (t0, n, cut) in enumerate(CHUNKS):
            src = raw[c][:].rearrange("p j (t i) -> p t j i", i=4)
            dst = grouped[c][:].rearrange("p (t i) j -> p t j i", i=4)
            nc.vector.tensor_copy(out=dst[:, 0 : cut // 4], in_=src[:, 0 : cut // 4])
            nc.scalar.copy(out=dst[:, cut // 4 : n // 4], in_=src[:, cut // 4 : n // 4])
            for q0, qn in QUANTS[t0]:
                cols = slice(t0 + q0, t0 + q0 + qn)
                nc.vector.quantize_mx(
                    out=words[:, cols].bitcast(FP8X4),
                    scales=scales[:, cols],
                    in_=grouped[c][:, q0 : q0 + qn, :].rearrange("p t j -> p (t j)"),
                )

        def experts(nbs, e0, e1):
            accs = [psum.tile([P, 4 * C], F32, name=f"acc", tag="acc") for nb in nbs]
            for nb, acc in zip(nbs, accs):
                for e in range(e0, e1):
                    feat = slice(nb * P, (nb + 1) * P)
                    slots = slice(e * C, (e + 1) * C)
                    nc.tensor.matmul_mx(
                        out=acc[:, (e - e0) * C : (e - e0 + 1) * C],
                        lhsT=w_sb[:, e, feat].bitcast(FP8X4),
                        lhsT_scale=ws_sb[4 * (e % 4) : P, e // 4 * N + nb * P : e // 4 * N + (nb + 1) * P],
                        rhs=slot_words[:, slots].bitcast(FP8X4),
                        rhs_scale=slot_scales[:, slots],
                        start=True,
                        stop=True,
                    )
            for nb, acc in zip(nbs, accs):
                for e in range(e0, e1):
                    nc.scalar.activation(
                        y[nb][:, e * C : (e + 1) * C],
                        acc[:, (e - e0) * C : (e - e0 + 1) * C],
                        GELU,
                        bias=b_sb[:, nb, e : e + 1],
                    )

        def pick(dst, src, s0, s1):
            nc.vector.tensor_copy(dst[:, s0:s1], src[:].indirect(offs_sb[:, s0 // 16 : s1 // 16]))

        for s0, s1, e0, e1 in SCALE_CUTS:
            if s0 in WORD_CUTS:
                pick(slot_words, words, s0, WORD_CUTS[s0])
            pick(slot_scales, scales, s0, s1)
            for a in range(e0, e1, 4):
                experts((0,), a, min(a + 4, e1))
        for nbs in ((1,), (2,), (3,)):
            for e0, e1 in LOADS:
                experts(nbs, e0, e1)

        def fetch(nb, t0, t1, r):
            part = keep.tile([P, t1 - t0], F32, name=f"part{nb}_{t0}_{r}")
            nc.vector.tensor_tensor(
                part[:],
                y[nb][:].indirect(pos_sb[r][:, t0 // 16 : t1 // 16]),
                gate_sb[r][:, t0:t1],
                MULT,
            )
            return part

        def add_by_identity(part, a, z, total):
            both = psum.tile([P, 4 * C], F32, name="both", tag="acc")
            for r in range(2):
                nc.tensor.matmul(both[:, 0 : z - a], ident[:], part[r][:, a:z], start=(r == 0), stop=(r == 1))
            nc.scalar.copy(total[:, a:z], both[:, 0 : z - a])

        def add_turned(part, a, z):
            turned = psum.tile([P, 4 * C], F32, name="turned", tag="acc")
            for t in range(a, z, P):
                for r in range(2):
                    nc.tensor.matmul(
                        turned[:, t - a : t - a + P], part[r][:, t : t + P], ident[:],
                        start=(r == 0), stop=(r == 1), is_transpose=True,
                    )
            rows = turns.tile([P, 4 * C], F32, name="rows")
            nc.scalar.copy(rows[:, 0 : z - a], turned[:, 0 : z - a])
            return rows

        def turn_back(rows, a, z, total):
            both = psum.tile([P, 4 * C], F32, name="both", tag="acc")
            for t in range(0, z - a, P):
                nc.tensor.transpose(both[:, t : t + P], rows[:, t : t + P], ident[:])
            nc.scalar.copy(total[:, a:z], both[:, 0 : z - a])

        def finish(nb, t0, t1, ways, part):
            total = keep.tile([P, t1 - t0], F32, name=f"total{nb}_{t0}")
            turned = [add_turned(part, a, z) if way == "turn" else None for way, a, z in ways]
            for rows, (way, a, z) in zip(turned, ways):
                if way == "turn":
                    turn_back(rows, a, z, total)
                elif way == "identity":
                    add_by_identity(part, a, z, total)
                else:
                    nc.vector.tensor_tensor(total[:, a:z], part[0][:, a:z], part[1][:, a:z], ADD)
                queue = nc.sync if way == "vector" else nc.scalar
                queue.dma_start(out=out[nb * P : (nb + 1) * P, t0 + a : t0 + z], in_=total[:, a:z])

        pieces = [
            (0, 0, T, [("identity", 0, 384), ("turn", 384, T)]),
            (1, 0, T, [("turn", 0, 384), ("turn", 384, T)]),
            (2, 0, 384, [("turn", 0, 384)]),
            (2, 384, T, [("vector", 0, 384)]),
            (3, 0, 512, [("vector", 0, 512)]),
        ]
        last = None
        for piece in pieces:
            first = fetch(*piece[:3], 0)
            if last:
                finish(*last)
            last = (*piece, (first, fetch(*piece[:3], 1)))
        ends = ((512, 640), (640, T))
        firsts = [fetch(3, t0, t1, 0) for t0, t1 in ends]
        finish(*last)
        seconds = [fetch(3, t0, t1, 1) for t0, t1 in ends]
        for (t0, t1), first, second in zip(ends, firsts, seconds):
            finish(3, t0, t1, [("vector", 0, t1 - t0)], (first, second))
